import numpy as np, ml_dtypes
CORES = [7,15,23,39,47,63,71,79,87,95,119,127]
N = 12
import mx_ref
NC = 256
BF = ml_dtypes.bfloat16
def setup_inputs(rng):
    def f(*shape):
        return mx_ref.flush((rng.standard_normal(shape, dtype=np.float32) * np.exp2(rng.integers(-2, 3, shape[:-1] + (1,)))).astype(BF))
    return {"w": f(N, 128, 512), "x": f(N, 128, 4 * NC)}
def setup_inputs_blocks(rng):
    d = setup_inputs(rng)
    for k in ("w", "x"): d[k] = mx_ref.spread(d[k], rng, 4)
    return d
def setup_inputs_wide(rng):
    d = setup_inputs(rng)
    for k in ("w", "x"): d[k] = mx_ref.flush((d[k].astype(np.float32) * np.exp2(rng.integers(-10, 11, (N, 1, 1))).astype(np.float32)).astype(BF))
    return d
def reference(w, x):
    X = [mx_ref.quantize(x[j]) for j in range(N)]
    y = np.full((N, 128, N * NC), np.nan, np.float32)
    for r in range(N):
        qw = mx_ref.quantize(w[r])
        for j in range(r + 1):
            y[r][:, NC * j:NC * j + NC] = mx_ref.matmul(qw, X[j])
    return {"y": y}

from concourse.bass import DstId, RemoteDMATransfer
from concourse.mybir import dt, ActivationFunctionType

N = 12
NC = 256
BANK = 512
BANKS = 8

SCRATCH = {
    "xb": ("sbuf", [128, 4 * NC], "bfloat16"),
    "wb": ("sbuf", [128, 512], "bfloat16"),
    "wq": ("sbuf", [128, 128], "float8_e4m3fn_x4"),
    "ws": ("sbuf", [128, 128], "uint8"),
    "xq": ("sbuf", [128, N * NC], "float8_e4m3fn_x4"),
    "xs": ("sbuf", [128, N * NC], "uint8"),
    "yb": ("sbuf", [128, N * NC], "float32"),
    "ps": ("psum", [128, BANKS * BANK], "float32"),
}
SEMAPHORES = (["ldx", "ldw", "qx", "qw", "sent", "st"] + ["s%d" % j for j in range(N)] + ["c%d" % j for j in range(N)]
              + ["m%d" % k for k in range(N)] + ["e%d" % k for k in range(N)])

AIDES = (2, 2, 1, 1, 1, 0, 0, 0, 0, 0, 0, 0)
FEED, SEND, HOP = 0.5, 1.0, 0.6
CROWD = 1.0
PLAN = {}


def build_plan(cores, topo):
    n = len(cores)
    every = range(topo.CHIPS * topo.CORES_PER_CHIP)

    def on_chip(ch):
        return [c for c in every if topo.chip(c) == ch]

    def mate(ch):
        return [m for m in range(topo.CHIPS) if topo.mates(ch, m)][0]

    def aides(ch):
        far = on_chip(mate(ch))[0]
        own = [c for c in on_chip(ch) if c in cores]
        return sorted([c for c in on_chip(ch) if c not in cores and topo.may_write(c, far)],
                      key=lambda c: (bool(own) and topo.die(c) == topo.die(own[0]), c))

    free, est, sends, relays, crowd = {}, {}, [], [], {}
    for j in range(n - 1, -1, -1):
        src = cores[j]
        ch = topo.chip(src)
        est[(src, j)] = 0.0
        units = {}
        for r in range(j + 1, n):
            c = topo.chip(cores[r])
            units.setdefault(min(c, mate(c)), []).append(cores[r])
        targets = []
        for ds in units.values():
            if len(ds) == 2:
                near = [d for d in ds if topo.same_plane(ch, topo.chip(d))][0]
                targets.append((0, -cores.index(ds[1]), near, ds))
            else:
                targets.append((1, -cores.index(ds[0]), ds[0], ds))
        t, team = 0.0, [src]
        for h in aides(ch)[:AIDES[j]]:
            sends.append([t, src, j, [h]])
            t += FEED
            est[(h, j)] = free[h] = t + HOP
            team.append(h)
        free[src] = t
        for kind, _, probe, ds in sorted(targets):
            s = min([s for s in team if topo.may_write(s, probe)],
                    key=lambda s: free[s] + CROWD * crowd.get((topo.chip(probe), topo.die(s)), 0))
            door = (topo.chip(probe), topo.die(s))
            crowd[door] = crowd.get(door, 0) + 1
            item = [free[s], s, j, ds]
            free[s] += SEND
            sends.append(item)
            if kind:
                est[(probe, j)] = free[s] + HOP
            else:
                relays.append((free[s] + HOP, j, probe, ds, item))
    for arrive, j, near, ds, item in sorted(relays, key=lambda x: x[:2]):
        q = min(aides(topo.chip(near))[::-1], key=lambda c: max(free.get(c, 0.0), arrive))
        item[3] = [q]
        est[(q, j)] = arrive
        start = max(free.get(q, 0.0), arrive)
        free[q] = start + SEND
        sends.append([start, q, j, ds])
        for d in ds:
            est[(d, j)] = free[q] + HOP
    ops, need = {}, {}
    for start, s, j, ds in sorted(sends, key=lambda x: x[:3]):
        used, tr = 0, []
        for d in sorted(ds, key=lambda d: topo.chip(d) == topo.chip(s)):
            m = topo.mask(s, d) & ~used
            used |= m
            tr.append((m, d))
            need[(d, j)] = bin(m).count("1")
        ops.setdefault(s, []).append((j, tr))
    order = [sorted(range(r + 1), key=lambda j: est[(cores[r], j)]) for r in range(n)]
    return ops, need, order, est


def rank_program(g, core, T, topo):
    cores = list(T.cores)
    if "p" not in PLAN:
        PLAN["p"] = build_plan(cores, topo)
    ops, need, order, _ = PLAN["p"]
    rank = T.rank_of(core)
    sem = T.sem

    def cols(j):
        return slice(j * NC, (j + 1) * NC)

    def wait(q, j, part):
        if j == rank:
            q.wait_ge(sem.qx, 1)
        else:
            q.wait_ge(sem["%s%d" % (part, j)], need[(core, j)])

    if rank is not None:
        g.sync.dma_start(T.xb[:], T.x[:]).then_inc(sem.ldx, 16)
        g.sync.dma_start(T.wb[:], T.w[:]).then_inc(sem.ldw, 16)
        g.vector.wait_ge(sem.ldx, 16)
        g.vector.quantize_mx(T.xq[:, cols(rank)], T.xs[:, cols(rank)], T.xb[:]).then_inc(sem.qx, 1)
        g.vector.wait_ge(sem.ldw, 16)
        g.vector.quantize_mx(T.wq[:], T.ws[:], T.wb[:]).then_inc(sem.qw, 1)

    sent = 0
    for j, tr in ops.get(core, []):
        for part in "sc":
            wait(g, j, part)
            ap = T.xs[:, cols(j)] if part == "s" else T.xq[:, cols(j)].bitcast(dt.uint8)
            there = sem["%s%d" % (part, j)]
            if len(tr) == 1:
                m, d = tr[0]
                rid, pid, _ = topo.addr(d)
                g.remote_dma(ap, ap, there, sem.sent, pid, rid, m)
            else:
                g.remote_dma_fused([RemoteDMATransfer(dst_ids=[DstId(rid=topo.addr(d)[0], pnc=topo.addr(d)[1])], dma_engine_mask=m,
                                                      remote_sem=there, src=ap, dst=ap) for m, d in tr], local_sem=sem.sent)
            sent += sum(bin(m).count("1") for m, d in tr)
    if sent:
        g.wait_ge(sem.sent, sent)

    if rank is None:
        return
    g.tensor.wait_ge(sem.qw, 1)
    for k, j in enumerate(order[rank]):
        wait(g.tensor, j, "s")
        if j != rank:
            wait(g.tensor, j, "c")
        if k >= BANKS:
            g.tensor.wait_ge(sem["e%d" % (k - BANKS)], 1)
        acc = T.ps[:, (k % BANKS) * BANK:(k % BANKS) * BANK + NC]
        g.tensor.matmul_mx(acc, T.wq[:], T.ws[:], T.xq[:, cols(j)], T.xs[:, cols(j)], True, True).then_inc(sem["m%d" % k], 1)
        if k % 2 == 0:
            g.vector.wait_ge(sem["m%d" % k], 1)
            g.vector.tensor_copy(T.yb[:, cols(j)], acc).then_inc(sem["e%d" % k], 1)
        else:
            g.scalar.wait_ge(sem["m%d" % k], 1)
            g.scalar.activation(T.yb[:, cols(j)], acc, ActivationFunctionType.Copy).then_inc(sem["e%d" % k], 1)
        g.sync.wait_ge(sem["e%d" % k], 1)
        g.sync.dma_start(T.y[:, cols(j)], T.yb[:, cols(j)]).then_inc(sem.st, 16)
    g.sync.wait_ge(sem.st, 16 * (rank + 1))
